import numpy as np
import ml_dtypes


def mxq(x, axis, fmt="e4m3"):
    dtype, down = {"e4m3": (ml_dtypes.float8_e4m3fn, 7), "e5m2": (ml_dtypes.float8_e5m2, 14)}[fmt]
    v = np.moveaxis(np.asarray(x, np.float32).astype(ml_dtypes.bfloat16).astype(np.float64), axis, -1)
    blocks = v.reshape(v.shape[:-1] + (-1, 32))
    amax = np.abs(blocks).max(-1, keepdims=True)
    byte = np.maximum(np.where(amax > 0, np.frexp(amax)[1] - 1 + 127, 0) - down, 1)
    scale = np.exp2(byte - 127.0)
    codes = (blocks / scale).astype(np.float32).astype(dtype).astype(np.float64)
    return np.moveaxis((codes * scale).reshape(v.shape), -1, axis)


WIDE = False


def mx_kscale(k):
    if not WIDE:
        return np.ones(k)
    levels = np.array([10, -10, 5, -5, 0])
    if k % 512:
        return np.exp2(np.random.permutation(np.resize(levels, k // 32))).repeat(32)
    a = np.empty((k // 512, 16))
    for p in range(k // 512):
        a[p, :8] = np.random.permutation(np.resize(levels, 8))
        for g in range(8):
            far = levels[np.abs(levels - a[p, g]) >= 10]
            a[p, g + 8] = far[np.random.randint(len(far))]
    return np.exp2(a.ravel()).repeat(32)


def f64(x):
    return np.asarray(x).astype(np.float64)


def striped(idx):
    return np.tile(np.asarray(idx).reshape(-1, 16).T, (8, 1)).astype(np.uint16)


def unstriped(offs):
    return offs[:16].T.reshape(-1).astype(np.int64)


E2M1 = np.array([0.0, 0.5, 1.0, 1.5, 2.0, 3.0, 4.0, 6.0, -0.0, -0.5, -1.0, -1.5, -2.0, -3.0, -4.0, -6.0])


def pack_weight(w, fmt):
    k, n = w.shape
    w = f64(np.asarray(w, np.float32).astype(ml_dtypes.bfloat16)).reshape(k // 32, 32, n)
    amax = np.abs(w).max(1)
    if fmt == "e4m3":
        byte = np.frexp(amax)[1] - 1 + 127 - 7
    else:
        mant, ex = np.frexp(amax / 6.0)
        byte = np.where(mant > 0.5, ex, ex - 1) + 127
    byte = np.clip(np.where(amax > 0, byte, 1), 1, 254)
    scaled = (w * np.exp2(127.0 - byte)[:, None, :]).reshape(k, n).astype(np.float32)
    by_word = np.ascontiguousarray(scaled.reshape(k // 512, 128, 4, n).transpose(0, 1, 3, 2))
    if fmt == "e4m3":
        words = by_word.astype(ml_dtypes.float8_e4m3fn).view(np.uint8)
    else:
        c = by_word.astype(ml_dtypes.float4_e2m1fn).view(np.uint8) & 0xF
        words = (c[..., 0::2] | (c[..., 1::2] << 4)).reshape(k // 512, 128, 2 * n)
    return np.ascontiguousarray(words), np.ascontiguousarray(byte.astype(np.uint8).reshape(k // 512, 16, n))


def unpack_weight(words, scales, fmt):
    g, _, n = scales.shape
    words = np.ascontiguousarray(words).reshape(g, 128, n, -1)
    if fmt == "e4m3":
        vals = words.view(ml_dtypes.float8_e4m3fn).astype(np.float64)
    else:
        nib = np.empty((g, 128, n, 4), np.uint8)
        nib[..., 0::2] = words & 0xF
        nib[..., 1::2] = words >> 4
        vals = E2M1[nib]
    vals = vals * np.repeat(np.exp2(scales.astype(np.float64) - 127.0), 8, axis=1)[..., None]
    return vals.transpose(0, 1, 3, 2).reshape(g * 512, n)


def bf(x):
    return np.asarray(x, np.float32).astype(ml_dtypes.bfloat16)


def planes(Y):
    r, m = Y.shape
    b = f64(bf(Y)).reshape(r // 32, 32, m)
    amax = np.abs(b).max(1)
    byte = np.clip(np.where(amax > 0, np.frexp(amax)[1] - 1 + 127 - 7, 1), 1, 254)
    codes = (b * np.exp2(127.0 - byte)[:, None, :]).reshape(r, m).astype(np.float32).astype(ml_dtypes.float8_e4m3fn).view(np.uint8)
    words = codes.reshape(r // 512, 128, 4, m).transpose(0, 1, 3, 2)
    return np.ascontiguousarray(words), np.ascontiguousarray(byte.astype(np.uint8).reshape(r // 512, 16, m))


D, T, I, Q, E, M = 512, 2048, 512, 256, 512, 1024


def setup_inputs():
    n = np.random.standard_normal
    idx = np.random.permutation(T)[:I]
    idx2 = np.random.permutation(T)[:I]
    idx3 = np.random.permutation(M)[:Q]
    fd = mx_kscale(D)
    fi = mx_kscale(I)
    ti = np.ones(T)
    ti[idx] = fi
    keysp = pack_weight(n((D, T)) / fd[:, None], "e2m1")
    return {
        "query": (n((D, Q)) * 1.0 / np.sqrt(D) * fd[:, None]).astype(np.float32),
        "keys_words": keysp[0],
        "keys_scales": keysp[1],
        "os": (np.random.uniform(0.02, 0.08, (1, I)) * fi).astype(np.float32),
        "vals": (n((E, T)) / ti).astype(np.float32),
        "member": (n((E, M))).astype(np.float32),
        "mgain": np.tile(np.random.uniform(0.5, 2.0, M), (128, 1)).astype(np.float32),
        "offs": striped(idx),
        "offs2": striped(idx2),
        "offs3": striped(idx3),
    }


def reference(query, keys_words, keys_scales, os, vals, member, mgain, offs, offs2, offs3):
    idx = unstriped(offs)
    idx2 = unstriped(offs2)
    idx3 = unstriped(offs3)
    keysu = unpack_weight(keys_words, keys_scales, "e2m1")
    queryq = mxq(f64(query), 0, "e4m3")
    a = queryq.T @ keysu
    s = a[:, idx] - a[:, idx2]
    w = np.maximum(s, 0.0)
    wo1 = w * f64(os)
    wt1 = wo1.T
    vt1 = f64(vals)[:, idx].T
    vt1q = mxq(vt1, 0, "e4m3")
    wt1q = mxq(wt1, 0, "e4m3")
    o = vt1q.T @ wt1q
    y = o * f64(mgain)[:1][:, idx3] + f64(member)[:, idx3]
    words, scales = planes(y)
    return y, words, scales

@@ -1,0 +1,214 @@
+from contextlib import ExitStack
+
+import concourse.mybir as mybir
+from concourse.masks import make_identity
+
+D, T, SLOTS, Q, E, M = 512, 2048, 512, 256, 512, 1024
+FLOPS = 2 * D * Q * T + 2 * SLOTS * E * Q
+
+F32 = mybir.dt.float32
+BF16 = mybir.dt.bfloat16
+I32 = mybir.dt.int32
+U32 = mybir.dt.uint32
+U16 = mybir.dt.uint16
+U8 = mybir.dt.uint8
+FP8X4 = mybir.dt.float8_e4m3fn_x4
+FP4X4 = mybir.dt.float4_e2m1fn_x4
+ALU = mybir.AluOpType
+COPY = mybir.ActivationFunctionType.Copy
+
+P = 128
+PACK = 4
+BANK = 512
+HALVES = Q // P
+
+
+def tile_attend_difference_bymember_lean_pl_kernel(
+    tc, query, keys_words, keys_scales, slot_factor, vals, member, mgain, offs, offs2, offs3, out_0, out_1, out_2
+):
+    nc = tc.nc
+    with ExitStack() as ctx:
+        sb = ctx.enter_context(tc.tile_pool(name="sb", bufs=1))
+        ps = ctx.enter_context(tc.psum_pool(name="ps", bufs=4))
+
+        first = sb.tile([P, SLOTS // 16], U16, name="first")
+        second = sb.tile([P, SLOTS // 16], U16, name="second")
+        third = sb.tile([P, Q // 16], U16, name="third")
+        q_raw = sb.tile([P, PACK, Q], F32, name="q_raw")
+        k_words = sb.tile([P, 2 * T], U8, name="k_words", align_bytes=64)
+        k_scales = sb.tile([P, T], U8, name="k_scales", align_bytes=64)
+        gain_row = sb.tile([P, M], F32, name="gain_row")
+        factor = sb.tile([P, PACK], F32, name="factor")
+        v_pool = [sb.tile([P, T], F32, name=f"v_pool{j}") for j in range(PACK)]
+        m_pool = [sb.tile([P, M], F32, name=f"m_pool{j}") for j in range(PACK)]
+        ident = sb.tile([P, P], F32, name="ident")
+
+        vals_dealt = vals.rearrange("(p j) t -> p j t", j=PACK)
+        member_dealt = member.rearrange("(p j) m -> p j m", j=PACK)
+        out_dealt = out_0.rearrange("(p j) q -> p j q", j=PACK)
+
+        nc.vector.memset(k_scales[:].bitcast(I32), 0)
+        nc.gpsimd.memset(gain_row[:], 0.0)
+        make_identity(nc, ident[:])
+
+        nc.sync.dma_start(out=q_raw[:], in_=query.rearrange("(p j) q -> p j q", j=PACK))
+        for g in range(4):
+            nc.sync.dma_start(
+                out=k_scales[32 * g : 32 * g + 4, :].bitcast(I32),
+                in_=keys_scales[0, 4 * g : 4 * g + 4, :].bitcast(I32),
+            )
+        nc.sync.dma_start(out=k_words[:].bitcast(I32), in_=keys_words[0].bitcast(I32))
+        nc.sync.dma_start(third[:], offs3)
+        nc.sync.dma_start(out=v_pool[0][:], in_=vals_dealt[:, 0, :])
+        nc.scalar.dma_start(out=gain_row[0:1, :], in_=mgain[0:1, :])
+        nc.sync.dma_start(first[:], offs)
+        nc.sync.dma_start(second[:], offs2)
+        nc.sync.dma_start(out=v_pool[1][:], in_=vals_dealt[:, 1, :])
+        nc.sync.dma_start(out=factor[:], in_=slot_factor.rearrange("o (p t) -> p (o t)", t=PACK))
+        for j in range(2, PACK):
+            nc.sync.dma_start(out=v_pool[j][:], in_=vals_dealt[:, j, :])
+        for j in range(PACK):
+            nc.sync.dma_start(out=m_pool[j][:], in_=member_dealt[:, j, :])
+
+        q_bf = [sb.tile([P, P, PACK], BF16, name=f"q_bf{h}", align_bytes=64) for h in range(HALVES)]
+        q_codes = sb.tile([P, Q], U32, name="q_codes", align_bytes=64)
+        q_scales = sb.tile([P, Q], U8, name="q_scales", align_bytes=64)
+        nc.vector.tensor_copy(out=q_bf[0][:], in_=q_raw[:, :, 0:P].rearrange("p j q -> p q j"))
+        nc.scalar.copy(out=q_bf[1][:], in_=q_raw[:, :, P:Q].rearrange("p j q -> p q j"))
+        for h in range(HALVES):
+            rows = slice(h * P, (h + 1) * P)
+            nc.vector.quantize_mx(
+                out=q_codes[:, rows].bitcast(FP8X4),
+                scales=q_scales[:, rows],
+                in_=q_bf[h][:].rearrange("p q j -> p (q j)"),
+            )
+
+        gain_listed = sb.tile([P, Q], F32, name="gain_listed")
+        gain_col = sb.tile([P, HALVES], F32, name="gain_col")
+        gain = sb.tile([P, Q], F32, name="gain")
+        nc.scalar.activation(gain_listed[:], gain_row[:].indirect(third[:]), COPY)
+        down = ps.tile([P, HALVES, P], F32, name="down", tag="turn")
+        for h in range(HALVES):
+            nc.tensor.transpose(down[:, h, :], gain_listed[:, h * P : (h + 1) * P], ident[:])
+        nc.scalar.copy(out=gain_col[:], in_=down[:, :, 0])
+        across = ps.tile([P, HALVES, P], F32, name="across", tag="turn")
+        for h in range(HALVES):
+            nc.tensor.transpose(across[:, h, :], gain_col[:, h : h + 1].to_broadcast([P, P]), ident[:])
+        nc.scalar.copy(out=gain[:], in_=across[:].rearrange("p h q -> p (h q)"))
+
+        scores = [sb.tile([P, T], F32, name=f"scores{h}") for h in range(HALVES)]
+        for h in range(HALVES):
+            rows = slice(h * P, (h + 1) * P)
+            for n in range(T // BANK):
+                cols = slice(n * BANK, (n + 1) * BANK)
+                acc = ps.tile([P, BANK], F32, name="acc", tag="acc")
+                nc.tensor.matmul_mx(
+                    out=acc[:],
+                    lhsT=q_codes[:, rows].bitcast(FP8X4),
+                    lhsT_scale=q_scales[:, rows],
+                    rhs=k_words[:, 2 * n * BANK : 2 * (n + 1) * BANK].bitcast(FP4X4),
+                    rhs_scale=k_scales[:, cols],
+                    start=True,
+                    stop=True,
+                )
+                if n % 2 == 0:
+                    nc.vector.tensor_copy(out=scores[h][:, cols], in_=acc[:])
+                else:
+                    nc.scalar.copy(out=scores[h][:, cols], in_=acc[:])
+
+        w_codes = sb.tile([P, Q], U32, name="w_codes", align_bytes=64)
+        w_scales = sb.tile([P, Q], U8, name="w_scales", align_bytes=64)
+        diffs = []
+        for h in range(HALVES):
+            minus = sb.tile([P, SLOTS], F32, name=f"minus{h}")
+            diff = sb.tile([P, SLOTS], F32, name=f"diff{h}")
+            nc.scalar.activation(minus[:], scores[h][:].indirect(second[:]), COPY)
+            nc.vector.tensor_tensor(diff[:], scores[h][:].indirect(first[:]), minus[:], ALU.subtract)
+            diffs.append(diff)
+        w_bf = []
+        for h in range(HALVES):
+            turned = ps.tile([P, PACK, P], F32, name="turned", tag="turn")
+            for t in range(PACK):
+                nc.tensor.transpose(turned[:, t, :], diffs[h][:, t::PACK], ident[:])
+            wb = sb.tile([P, P, PACK], BF16, name=f"w_bf{h}", align_bytes=64)
+            nc.vector.scalar_tensor_tensor(
+                out=wb[:],
+                in0=turned[:].rearrange("p t q -> p q t"),
+                scalar=0.0,
+                in1=factor[:].unsqueeze(1).to_broadcast([P, P, PACK]),
+                op0=ALU.max,
+                op1=ALU.mult,
+            )
+            w_bf.append(wb)
+        for h in range(HALVES):
+            rows = slice(h * P, (h + 1) * P)
+            nc.vector.quantize_mx(
+                out=w_codes[:, rows].bitcast(FP8X4),
+                scales=w_scales[:, rows],
+                in_=w_bf[h][:].rearrange("p q t -> p (q t)"),
+            )
+
+        y = sb.tile([P, PACK, Q], F32, name="y")
+        scaled = []
+        for j in range(PACK):
+            listed = sb.tile([P, SLOTS], BF16, name=f"v_listed{j}")
+            nc.scalar.activation(listed[:], v_pool[j][:].indirect(first[:]), COPY)
+            pairs = listed[:].bitcast(F32)
+            v_turned = ps.tile([P, 2, P], F32, name="v_turned", tag="turn")
+            for u in range(2):
+                nc.tensor.transpose(v_turned[:, u, :], pairs[:, u::2], ident[:])
+            v_bf = sb.tile([P, P * PACK], BF16, name=f"v_bf{j}", align_bytes=64)
+            nc.scalar.copy(
+                out=v_bf[:].bitcast(F32).rearrange("p (e u) -> p e u", u=2),
+                in_=v_turned[:].rearrange("p u e -> p e u"),
+            )
+            v_codes = sb.tile([P, P], U32, name=f"v_codes{j}", align_bytes=64)
+            v_scales = sb.tile([P, P], U8, name=f"v_scales{j}", align_bytes=64)
+            nc.vector.quantize_mx(out=v_codes[:].bitcast(FP8X4), scales=v_scales[:], in_=v_bf[:])
+            acc = ps.tile([P, Q], F32, name="acc", tag="acc")
+            nc.tensor.matmul_mx(
+                out=acc[:],
+                lhsT=v_codes[:].bitcast(FP8X4),
+                lhsT_scale=v_scales[:],
+                rhs=w_codes[:].bitcast(FP8X4),
+                rhs_scale=w_scales[:],
+                start=True,
+                stop=True,
+            )
+            sc = sb.tile([P, Q], F32, name=f"scaled{j}")
+            nc.vector.tensor_tensor(sc[:], acc[:], gain[:], ALU.mult)
+            scaled.append(sc)
+
+        last = PACK - 1
+        for j in range(last):
+            nc.vector.tensor_tensor(y[:, j, :], m_pool[j][:].indirect(third[:]), scaled[j][:], ALU.add)
+            if j == 1:
+                nc.sync.dma_start(out=out_dealt[:, 0:2, :], in_=y[:, 0:2, :])
+        nc.sync.dma_start(out=out_dealt[:, 2, :], in_=y[:, 2, :])
+        for h in range(HALVES):
+            rows = slice(h * P, (h + 1) * P)
+            part = third[:, h * (P // 16) : (h + 1) * (P // 16)]
+            nc.vector.tensor_tensor(y[:, last, rows], m_pool[last][:].indirect(part), scaled[last][:, rows], ALU.add)
+        nc.sync.dma_start(out=out_dealt[:, last, :], in_=y[:, last, :])
+
+        y_codes = sb.tile([P, Q], U32, name="y_codes", align_bytes=64)
+        y_scales = sb.tile([P, Q], U8, name="y_scales", align_bytes=64)
+        y_bf = [sb.tile([P, P, PACK], BF16, name=f"y_bf{h}", align_bytes=64) for h in range(HALVES)]
+        for h in range(HALVES):
+            nc.vector.tensor_copy(out=y_bf[h][:], in_=y[:, :, h * P : (h + 1) * P].rearrange("p j q -> p q j"))
+        for h in range(HALVES):
+            rows = slice(h * P, (h + 1) * P)
+            nc.vector.quantize_mx(
+                out=y_codes[:, rows].bitcast(FP8X4),
+                scales=y_scales[:, rows],
+                in_=y_bf[h][:].rearrange("p q j -> p (q j)"),
+            )
+        nc.sync.dma_start(
+            out=out_1.rearrange("z p c r -> p (z c r)").bitcast(I32), in_=y_codes[:].bitcast(I32)
+        )
+        for g in range(4):
+            queue = nc.scalar if g % 2 == 0 else nc.sync
+            queue.dma_start(
+                out=out_2[0, 4 * g : 4 * g + 4, :].bitcast(I32),
+                in_=y_scales[32 * g : 32 * g + 4, :].bitcast(I32),
+            )

@@ -29,13 +29,13 @@ def tile_attend_difference_bymember_lean_pl_kernel(
     nc = tc.nc
     with ExitStack() as ctx:
         sb = ctx.enter_context(tc.tile_pool(name="sb", bufs=1))
-        ps = ctx.enter_context(tc.psum_pool(name="ps", bufs=4))
+        ps = ctx.enter_context(tc.psum_pool(name="ps", bufs=1))
 
         first = sb.tile([P, SLOTS // 16], U16, name="first")
         second = sb.tile([P, SLOTS // 16], U16, name="second")
         third = sb.tile([P, Q // 16], U16, name="third")
         q_raw = sb.tile([P, PACK, Q], F32, name="q_raw")
-        k_words = sb.tile([P, 2 * T], U8, name="k_words", align_bytes=64)
+        k_words = [sb.tile([P, T], U8, name=f"k_words{i}", align_bytes=64) for i in range(2)]
         k_scales = sb.tile([P, T], U8, name="k_scales", align_bytes=64)
         gain_row = sb.tile([P, M], F32, name="gain_row")
         factor = sb.tile([P, PACK], F32, name="factor")
@@ -48,7 +48,6 @@ def tile_attend_difference_bymember_lean_pl_kernel(
         out_dealt = out_0.rearrange("(p j) q -> p j q", j=PACK)
 
         nc.vector.memset(k_scales[:].bitcast(I32), 0)
-        nc.gpsimd.memset(gain_row[:], 0.0)
         make_identity(nc, ident[:])
 
         nc.sync.dma_start(out=q_raw[:], in_=query.rearrange("(p j) q -> p j q", j=PACK))
@@ -57,18 +56,21 @@ def tile_attend_difference_bymember_lean_pl_kernel(
                 out=k_scales[32 * g : 32 * g + 4, :].bitcast(I32),
                 in_=keys_scales[0, 4 * g : 4 * g + 4, :].bitcast(I32),
             )
-        nc.sync.dma_start(out=k_words[:].bitcast(I32), in_=keys_words[0].bitcast(I32))
-        nc.sync.dma_start(third[:], offs3)
+        for i in range(2):
+            nc.sync.dma_start(out=k_words[i][:].bitcast(I32), in_=keys_words[0, :, i * T : (i + 1) * T].bitcast(I32))
         nc.sync.dma_start(out=v_pool[0][:], in_=vals_dealt[:, 0, :])
-        nc.scalar.dma_start(out=gain_row[0:1, :], in_=mgain[0:1, :])
-        nc.sync.dma_start(first[:], offs)
         nc.sync.dma_start(second[:], offs2)
+        nc.sync.dma_start(first[:], offs)
+        nc.sync.dma_start(third[:], offs3)
         nc.sync.dma_start(out=v_pool[1][:], in_=vals_dealt[:, 1, :])
         nc.sync.dma_start(out=factor[:], in_=slot_factor.rearrange("o (p t) -> p (o t)", t=PACK))
-        for j in range(2, PACK):
-            nc.sync.dma_start(out=v_pool[j][:], in_=vals_dealt[:, j, :])
-        for j in range(PACK):
-            nc.sync.dma_start(out=m_pool[j][:], in_=member_dealt[:, j, :])
+        nc.sync.dma_start(out=v_pool[2][:], in_=vals_dealt[:, 2, :])
+        nc.sync.dma_start(out=v_pool[3][:], in_=vals_dealt[:, 3, :])
+        nc.sync.dma_start(out=gain_row[:], in_=mgain)
+        nc.sync.dma_start(out=m_pool[0][:], in_=member_dealt[:, 0, :])
+        nc.sync.dma_start(out=m_pool[1][:], in_=member_dealt[:, 1, :])
+        nc.sync.dma_start(out=m_pool[2][:], in_=member_dealt[:, 2, :])
+        nc.sync.dma_start(out=m_pool[3][:], in_=member_dealt[:, 3, :])
 
         q_bf = [sb.tile([P, P, PACK], BF16, name=f"q_bf{h}", align_bytes=64) for h in range(HALVES)]
         q_codes = sb.tile([P, Q], U32, name="q_codes", align_bytes=64)
@@ -83,35 +85,22 @@ def tile_attend_difference_bymember_lean_pl_kernel(
                 in_=q_bf[h][:].rearrange("p q j -> p (q j)"),
             )
 
-        gain_listed = sb.tile([P, Q], F32, name="gain_listed")
-        gain_col = sb.tile([P, HALVES], F32, name="gain_col")
-        gain = sb.tile([P, Q], F32, name="gain")
-        nc.scalar.activation(gain_listed[:], gain_row[:].indirect(third[:]), COPY)
-        down = ps.tile([P, HALVES, P], F32, name="down", tag="turn")
-        for h in range(HALVES):
-            nc.tensor.transpose(down[:, h, :], gain_listed[:, h * P : (h + 1) * P], ident[:])
-        nc.scalar.copy(out=gain_col[:], in_=down[:, :, 0])
-        across = ps.tile([P, HALVES, P], F32, name="across", tag="turn")
-        for h in range(HALVES):
-            nc.tensor.transpose(across[:, h, :], gain_col[:, h : h + 1].to_broadcast([P, P]), ident[:])
-        nc.scalar.copy(out=gain[:], in_=across[:].rearrange("p h q -> p (h q)"))
-
         scores = [sb.tile([P, T], F32, name=f"scores{h}") for h in range(HALVES)]
         for h in range(HALVES):
             rows = slice(h * P, (h + 1) * P)
             for n in range(T // BANK):
                 cols = slice(n * BANK, (n + 1) * BANK)
-                acc = ps.tile([P, BANK], F32, name="acc", tag="acc")
+                acc = ps.tile([P, BANK], F32, name="acc", tag="acc", bufs=4)
                 nc.tensor.matmul_mx(
                     out=acc[:],
                     lhsT=q_codes[:, rows].bitcast(FP8X4),
                     lhsT_scale=q_scales[:, rows],
-                    rhs=k_words[:, 2 * n * BANK : 2 * (n + 1) * BANK].bitcast(FP4X4),
+                    rhs=k_words[n // 2][:, 2 * (n % 2) * BANK : 2 * (n % 2 + 1) * BANK].bitcast(FP4X4),
                     rhs_scale=k_scales[:, cols],
                     start=True,
                     stop=True,
                 )
-                if n % 2 == 0:
+                if "SSVVVVVV"[4 * h + n] == "V":
                     nc.vector.tensor_copy(out=scores[h][:, cols], in_=acc[:])
                 else:
                     nc.scalar.copy(out=scores[h][:, cols], in_=acc[:])
@@ -127,7 +116,7 @@ def tile_attend_difference_bymember_lean_pl_kernel(
             diffs.append(diff)
         w_bf = []
         for h in range(HALVES):
-            turned = ps.tile([P, PACK, P], F32, name="turned", tag="turn")
+            turned = ps.tile([P, PACK, P], F32, name="turned", tag=f"turn{h}")
             for t in range(PACK):
                 nc.tensor.transpose(turned[:, t, :], diffs[h][:, t::PACK], ident[:])
             wb = sb.tile([P, P, PACK], BF16, name=f"w_bf{h}", align_bytes=64)
@@ -148,54 +137,68 @@ def tile_attend_difference_bymember_lean_pl_kernel(
                 in_=w_bf[h][:].rearrange("p q t -> p (q t)"),
             )
 
+        gain = sb.tile([P, Q], F32, name="gain")
+        nc.scalar.activation(gain[:], gain_row[:].indirect(third[:]), COPY)
+
         y = sb.tile([P, PACK, Q], F32, name="y")
-        scaled = []
-        for j in range(PACK):
-            listed = sb.tile([P, SLOTS], BF16, name=f"v_listed{j}")
-            nc.scalar.activation(listed[:], v_pool[j][:].indirect(first[:]), COPY)
-            pairs = listed[:].bitcast(F32)
-            v_turned = ps.tile([P, 2, P], F32, name="v_turned", tag="turn")
-            for u in range(2):
-                nc.tensor.transpose(v_turned[:, u, :], pairs[:, u::2], ident[:])
-            v_bf = sb.tile([P, P * PACK], BF16, name=f"v_bf{j}", align_bytes=64)
-            nc.scalar.copy(
-                out=v_bf[:].bitcast(F32).rearrange("p (e u) -> p e u", u=2),
-                in_=v_turned[:].rearrange("p u e -> p e u"),
+        v_quant = []
+        for pair in range(2):
+            v_turned = ps.tile([P, 2, 2, P], F32, name="v_turned", tag=f"late{pair}")
+            for i in range(2):
+                j = 2 * pair + i
+                listed = sb.tile([P, SLOTS], BF16, name=f"v_listed{j}")
+                nc.scalar.activation(listed[:], v_pool[j][:].indirect(first[:]), COPY)
+                words = listed[:].bitcast(F32)
+                for u in range(2):
+                    nc.tensor.transpose(v_turned[:, i, u, :], words[:, u::2], ident[:])
+            v_bf = sb.tile([P, 2 * P * PACK], BF16, name=f"v_bf{pair}", align_bytes=64)
+            nc.vector.tensor_copy(
+                out=v_bf[:].bitcast(F32).rearrange("p (i e u) -> p i e u", i=2, u=2),
+                in_=v_turned[:].rearrange("p i u e -> p i e u"),
             )
-            v_codes = sb.tile([P, P], U32, name=f"v_codes{j}", align_bytes=64)
-            v_scales = sb.tile([P, P], U8, name=f"v_scales{j}", align_bytes=64)
+            v_codes = sb.tile([P, 2 * P], U32, name=f"v_codes{pair}", align_bytes=64)
+            v_scales = sb.tile([P, 2 * P], U8, name=f"v_scales{pair}", align_bytes=64)
             nc.vector.quantize_mx(out=v_codes[:].bitcast(FP8X4), scales=v_scales[:], in_=v_bf[:])
-            acc = ps.tile([P, Q], F32, name="acc", tag="acc")
-            nc.tensor.matmul_mx(
-                out=acc[:],
-                lhsT=v_codes[:].bitcast(FP8X4),
-                lhsT_scale=v_scales[:],
-                rhs=w_codes[:].bitcast(FP8X4),
-                rhs_scale=w_scales[:],
-                start=True,
-                stop=True,
+            v_quant.append((v_codes, v_scales))
+
+        scaled = sb.tile([P, PACK, Q], F32, name="scaled")
+        for pair in range(2):
+            acc = ps.tile([P, 2, Q], F32, name="acc", tag=f"late{1 - pair}")
+            for i in range(2):
+                cols = slice(i * P, (i + 1) * P)
+                nc.tensor.matmul_mx(
+                    out=acc[:, i, :],
+                    lhsT=v_quant[pair][0][:, cols].bitcast(FP8X4),
+                    lhsT_scale=v_quant[pair][1][:, cols],
+                    rhs=w_codes[:].bitcast(FP8X4),
+                    rhs_scale=w_scales[:],
+                    start=True,
+                    stop=True,
+                )
+            nc.vector.tensor_tensor(
+                scaled[:, 2 * pair : 2 * pair + 2, :], acc[:], gain[:].unsqueeze(1).to_broadcast([P, 2, Q]), ALU.mult
             )
-            sc = sb.tile([P, Q], F32, name=f"scaled{j}")
-            nc.vector.tensor_tensor(sc[:], acc[:], gain[:], ALU.mult)
-            scaled.append(sc)
 
         last = PACK - 1
+        m_listed = sb.tile([P, last, Q], F32, name="m_listed")
         for j in range(last):
-            nc.vector.tensor_tensor(y[:, j, :], m_pool[j][:].indirect(third[:]), scaled[j][:], ALU.add)
-            if j == 1:
-                nc.sync.dma_start(out=out_dealt[:, 0:2, :], in_=y[:, 0:2, :])
+            nc.scalar.activation(m_listed[:, j, :], m_pool[j][:].indirect(third[:]), COPY)
+        nc.vector.tensor_tensor(y[:, 0:2, :], m_listed[:, 0:2, :], scaled[:, 0:2, :], ALU.add)
+        nc.sync.dma_start(out=out_dealt[:, 0:2, :], in_=y[:, 0:2, :])
+        nc.vector.tensor_tensor(y[:, 2, :], m_listed[:, 2, :], scaled[:, 2, :], ALU.add)
         nc.sync.dma_start(out=out_dealt[:, 2, :], in_=y[:, 2, :])
         for h in range(HALVES):
             rows = slice(h * P, (h + 1) * P)
             part = third[:, h * (P // 16) : (h + 1) * (P // 16)]
-            nc.vector.tensor_tensor(y[:, last, rows], m_pool[last][:].indirect(part), scaled[last][:, rows], ALU.add)
+            nc.vector.tensor_tensor(y[:, last, rows], m_pool[last][:].indirect(part), scaled[:, last, rows], ALU.add)
         nc.sync.dma_start(out=out_dealt[:, last, :], in_=y[:, last, :])
 
         y_codes = sb.tile([P, Q], U32, name="y_codes", align_bytes=64)
         y_scales = sb.tile([P, Q], U8, name="y_scales", align_bytes=64)
         y_bf = [sb.tile([P, P, PACK], BF16, name=f"y_bf{h}", align_bytes=64) for h in range(HALVES)]
         for h in range(HALVES):
-            nc.vector.tensor_copy(out=y_bf[h][:], in_=y[:, :, h * P : (h + 1) * P].rearrange("p j q -> p q j"))
+            cast = nc.vector.tensor_copy if "SV"[h] == "V" else nc.scalar.copy
+            cast(out=y_bf[h][:], in_=y[:, :, h * P : (h + 1) * P].rearrange("p j q -> p q j"))
         for h in range(HALVES):
             rows = slice(h * P, (h + 1) * P)
             nc.vector.quantize_mx(

from contextlib import ExitStack

import concourse.mybir as mybir
from concourse.masks import make_identity

D, T, SLOTS, Q, E, M = 512, 2048, 512, 256, 512, 1024
FLOPS = 2 * D * Q * T + 2 * SLOTS * E * Q

F32 = mybir.dt.float32
BF16 = mybir.dt.bfloat16
I32 = mybir.dt.int32
U32 = mybir.dt.uint32
U16 = mybir.dt.uint16
U8 = mybir.dt.uint8
FP8X4 = mybir.dt.float8_e4m3fn_x4
FP4X4 = mybir.dt.float4_e2m1fn_x4
ALU = mybir.AluOpType
COPY = mybir.ActivationFunctionType.Copy

P = 128
PACK = 4
BANK = 512
HALVES = Q // P


def tile_attend_difference_bymember_lean_pl_kernel(
    tc, query, keys_words, keys_scales, slot_factor, vals, member, mgain, offs, offs2, offs3, out_0, out_1, out_2
):
    nc = tc.nc
    with ExitStack() as ctx:
        sb = ctx.enter_context(tc.tile_pool(name="sb", bufs=1))
        ps = ctx.enter_context(tc.psum_pool(name="ps", bufs=1))

        first = sb.tile([P, SLOTS // 16], U16, name="first")
        second = sb.tile([P, SLOTS // 16], U16, name="second")
        third = sb.tile([P, Q // 16], U16, name="third")
        q_raw = sb.tile([P, PACK, Q], F32, name="q_raw")
        k_words = [sb.tile([P, T], U8, name=f"k_words{i}", align_bytes=64) for i in range(2)]
        k_scales = sb.tile([P, T], U8, name="k_scales", align_bytes=64)
        gain_row = sb.tile([P, M], F32, name="gain_row")
        factor = sb.tile([P, PACK], F32, name="factor")
        v_pool = [sb.tile([P, T], F32, name=f"v_pool{j}") for j in range(PACK)]
        m_pool = [sb.tile([P, M], F32, name=f"m_pool{j}") for j in range(PACK)]
        ident = sb.tile([P, P], F32, name="ident")

        vals_dealt = vals.rearrange("(p j) t -> p j t", j=PACK)
        member_dealt = member.rearrange("(p j) m -> p j m", j=PACK)
        out_dealt = out_0.rearrange("(p j) q -> p j q", j=PACK)

        nc.vector.memset(k_scales[:].bitcast(I32), 0)
        make_identity(nc, ident[:])

        nc.sync.dma_start(out=q_raw[:], in_=query.rearrange("(p j) q -> p j q", j=PACK))
        for g in range(4):
            nc.sync.dma_start(
                out=k_scales[32 * g : 32 * g + 4, :].bitcast(I32),
                in_=keys_scales[0, 4 * g : 4 * g + 4, :].bitcast(I32),
            )
        for i in range(2):
            nc.sync.dma_start(out=k_words[i][:].bitcast(I32), in_=keys_words[0, :, i * T : (i + 1) * T].bitcast(I32))
        nc.sync.dma_start(out=v_pool[0][:], in_=vals_dealt[:, 0, :])
        nc.sync.dma_start(second[:], offs2)
        nc.sync.dma_start(first[:], offs)
        nc.sync.dma_start(third[:], offs3)
        nc.sync.dma_start(out=v_pool[1][:], in_=vals_dealt[:, 1, :])
        nc.sync.dma_start(out=factor[:], in_=slot_factor.rearrange("o (p t) -> p (o t)", t=PACK))
        nc.sync.dma_start(out=v_pool[2][:], in_=vals_dealt[:, 2, :])
        nc.sync.dma_start(out=v_pool[3][:], in_=vals_dealt[:, 3, :])
        nc.sync.dma_start(out=gain_row[:], in_=mgain)
        nc.sync.dma_start(out=m_pool[0][:], in_=member_dealt[:, 0, :])
        nc.sync.dma_start(out=m_pool[1][:], in_=member_dealt[:, 1, :])
        nc.sync.dma_start(out=m_pool[2][:], in_=member_dealt[:, 2, :])
        nc.sync.dma_start(out=m_pool[3][:], in_=member_dealt[:, 3, :])

        q_bf = [sb.tile([P, P, PACK], BF16, name=f"q_bf{h}", align_bytes=64) for h in range(HALVES)]
        q_codes = sb.tile([P, Q], U32, name="q_codes", align_bytes=64)
        q_scales = sb.tile([P, Q], U8, name="q_scales", align_bytes=64)
        nc.vector.tensor_copy(out=q_bf[0][:], in_=q_raw[:, :, 0:P].rearrange("p j q -> p q j"))
        nc.scalar.copy(out=q_bf[1][:], in_=q_raw[:, :, P:Q].rearrange("p j q -> p q j"))
        for h in range(HALVES):
            rows = slice(h * P, (h + 1) * P)
            nc.vector.quantize_mx(
                out=q_codes[:, rows].bitcast(FP8X4),
                scales=q_scales[:, rows],
                in_=q_bf[h][:].rearrange("p q j -> p (q j)"),
            )

        scores = [sb.tile([P, T], F32, name=f"scores{h}") for h in range(HALVES)]
        for h in range(HALVES):
            rows = slice(h * P, (h + 1) * P)
            for n in range(T // BANK):
                cols = slice(n * BANK, (n + 1) * BANK)
                acc = ps.tile([P, BANK], F32, name="acc", tag="acc", bufs=4)
                nc.tensor.matmul_mx(
                    out=acc[:],
                    lhsT=q_codes[:, rows].bitcast(FP8X4),
                    lhsT_scale=q_scales[:, rows],
                    rhs=k_words[n // 2][:, 2 * (n % 2) * BANK : 2 * (n % 2 + 1) * BANK].bitcast(FP4X4),
                    rhs_scale=k_scales[:, cols],
                    start=True,
                    stop=True,
                )
                if "SSVVVVVV"[4 * h + n] == "V":
                    nc.vector.tensor_copy(out=scores[h][:, cols], in_=acc[:])
                else:
                    nc.scalar.copy(out=scores[h][:, cols], in_=acc[:])

        w_codes = sb.tile([P, Q], U32, name="w_codes", align_bytes=64)
        w_scales = sb.tile([P, Q], U8, name="w_scales", align_bytes=64)
        diffs = []
        for h in range(HALVES):
            minus = sb.tile([P, SLOTS], F32, name=f"minus{h}")
            diff = sb.tile([P, SLOTS], F32, name=f"diff{h}")
            nc.scalar.activation(minus[:], scores[h][:].indirect(second[:]), COPY)
            nc.vector.tensor_tensor(diff[:], scores[h][:].indirect(first[:]), minus[:], ALU.subtract)
            diffs.append(diff)
        w_bf = []
        for h in range(HALVES):
            turned = ps.tile([P, PACK, P], F32, name="turned", tag=f"turn{h}")
            for t in range(PACK):
                nc.tensor.transpose(turned[:, t, :], diffs[h][:, t::PACK], ident[:])
            wb = sb.tile([P, P, PACK], BF16, name=f"w_bf{h}", align_bytes=64)
            nc.vector.scalar_tensor_tensor(
                out=wb[:],
                in0=turned[:].rearrange("p t q -> p q t"),
                scalar=0.0,
                in1=factor[:].unsqueeze(1).to_broadcast([P, P, PACK]),
                op0=ALU.max,
                op1=ALU.mult,
            )
            w_bf.append(wb)
        for h in range(HALVES):
            rows = slice(h * P, (h + 1) * P)
            nc.vector.quantize_mx(
                out=w_codes[:, rows].bitcast(FP8X4),
                scales=w_scales[:, rows],
                in_=w_bf[h][:].rearrange("p q t -> p (q t)"),
            )

        gain = sb.tile([P, Q], F32, name="gain")
        nc.scalar.activation(gain[:], gain_row[:].indirect(third[:]), COPY)

        y = sb.tile([P, PACK, Q], F32, name="y")
        v_quant = []
        for pair in range(2):
            v_turned = ps.tile([P, 2, 2, P], F32, name="v_turned", tag=f"late{pair}")
            for i in range(2):
                j = 2 * pair + i
                listed = sb.tile([P, SLOTS], BF16, name=f"v_listed{j}")
                nc.scalar.activation(listed[:], v_pool[j][:].indirect(first[:]), COPY)
                words = listed[:].bitcast(F32)
                for u in range(2):
                    nc.tensor.transpose(v_turned[:, i, u, :], words[:, u::2], ident[:])
            v_bf = sb.tile([P, 2 * P * PACK], BF16, name=f"v_bf{pair}", align_bytes=64)
            nc.vector.tensor_copy(
                out=v_bf[:].bitcast(F32).rearrange("p (i e u) -> p i e u", i=2, u=2),
                in_=v_turned[:].rearrange("p i u e -> p i e u"),
            )
            v_codes = sb.tile([P, 2 * P], U32, name=f"v_codes{pair}", align_bytes=64)
            v_scales = sb.tile([P, 2 * P], U8, name=f"v_scales{pair}", align_bytes=64)
            nc.vector.quantize_mx(out=v_codes[:].bitcast(FP8X4), scales=v_scales[:], in_=v_bf[:])
            v_quant.append((v_codes, v_scales))

        scaled = sb.tile([P, PACK, Q], F32, name="scaled")
        for pair in range(2):
            acc = ps.tile([P, 2, Q], F32, name="acc", tag=f"late{1 - pair}")
            for i in range(2):
                cols = slice(i * P, (i + 1) * P)
                nc.tensor.matmul_mx(
                    out=acc[:, i, :],
                    lhsT=v_quant[pair][0][:, cols].bitcast(FP8X4),
                    lhsT_scale=v_quant[pair][1][:, cols],
                    rhs=w_codes[:].bitcast(FP8X4),
                    rhs_scale=w_scales[:],
                    start=True,
                    stop=True,
                )
            nc.vector.tensor_tensor(
                scaled[:, 2 * pair : 2 * pair + 2, :], acc[:], gain[:].unsqueeze(1).to_broadcast([P, 2, Q]), ALU.mult
            )

        last = PACK - 1
        m_listed = sb.tile([P, last, Q], F32, name="m_listed")
        for j in range(last):
            nc.scalar.activation(m_listed[:, j, :], m_pool[j][:].indirect(third[:]), COPY)
        nc.vector.tensor_tensor(y[:, 0:2, :], m_listed[:, 0:2, :], scaled[:, 0:2, :], ALU.add)
        nc.sync.dma_start(out=out_dealt[:, 0:2, :], in_=y[:, 0:2, :])
        nc.vector.tensor_tensor(y[:, 2, :], m_listed[:, 2, :], scaled[:, 2, :], ALU.add)
        nc.sync.dma_start(out=out_dealt[:, 2, :], in_=y[:, 2, :])
        for h in range(HALVES):
            rows = slice(h * P, (h + 1) * P)
            part = third[:, h * (P // 16) : (h + 1) * (P // 16)]
            nc.vector.tensor_tensor(y[:, last, rows], m_pool[last][:].indirect(part), scaled[:, last, rows], ALU.add)
        nc.sync.dma_start(out=out_dealt[:, last, :], in_=y[:, last, :])

        y_codes = sb.tile([P, Q], U32, name="y_codes", align_bytes=64)
        y_scales = sb.tile([P, Q], U8, name="y_scales", align_bytes=64)
        y_bf = [sb.tile([P, P, PACK], BF16, name=f"y_bf{h}", align_bytes=64) for h in range(HALVES)]
        for h in range(HALVES):
            cast = nc.vector.tensor_copy if "SV"[h] == "V" else nc.scalar.copy
            cast(out=y_bf[h][:], in_=y[:, :, h * P : (h + 1) * P].rearrange("p j q -> p q j"))
        for h in range(HALVES):
            rows = slice(h * P, (h + 1) * P)
            nc.vector.quantize_mx(
                out=y_codes[:, rows].bitcast(FP8X4),
                scales=y_scales[:, rows],
                in_=y_bf[h][:].rearrange("p q j -> p (q j)"),
            )
        nc.sync.dma_start(
            out=out_1.rearrange("z p c r -> p (z c r)").bitcast(I32), in_=y_codes[:].bitcast(I32)
        )
        for g in range(4):
            queue = nc.scalar if g % 2 == 0 else nc.sync
            queue.dma_start(
                out=out_2[0, 4 * g : 4 * g + 4, :].bitcast(I32),
                in_=y_scales[32 * g : 32 * g + 4, :].bitcast(I32),
            )
